import numpy as np
import ml_dtypes


def mxq(x, axis, fmt="e4m3"):
    dtype, down = {"e4m3": (ml_dtypes.float8_e4m3fn, 7), "e5m2": (ml_dtypes.float8_e5m2, 14)}[fmt]
    v = np.moveaxis(np.asarray(x, np.float32).astype(ml_dtypes.bfloat16).astype(np.float64), axis, -1)
    blocks = v.reshape(v.shape[:-1] + (-1, 32))
    amax = np.abs(blocks).max(-1, keepdims=True)
    byte = np.maximum(np.where(amax > 0, np.frexp(amax)[1] - 1 + 127, 0) - down, 1)
    scale = np.exp2(byte - 127.0)
    codes = (blocks / scale).astype(np.float32).astype(dtype).astype(np.float64)
    return np.moveaxis((codes * scale).reshape(v.shape), -1, axis)


WIDE = False


def mx_kscale(k):
    if not WIDE:
        return np.ones(k)
    levels = np.array([10, -10, 5, -5, 0])
    if k % 512:
        return np.exp2(np.random.permutation(np.resize(levels, k // 32))).repeat(32)
    a = np.empty((k // 512, 16))
    for p in range(k // 512):
        a[p, :8] = np.random.permutation(np.resize(levels, 8))
        for g in range(8):
            far = levels[np.abs(levels - a[p, g]) >= 10]
            a[p, g + 8] = far[np.random.randint(len(far))]
    return np.exp2(a.ravel()).repeat(32)


def f64(x):
    return np.asarray(x).astype(np.float64)


def striped8(idx):
    return np.asarray(idx).reshape(8, -1, 16).transpose(0, 2, 1).reshape(128, -1).astype(np.uint16)


def unstriped8(offs):
    return offs.reshape(8, 16, -1).transpose(0, 2, 1).reshape(8, -1).astype(np.int64)


def pick8(x, idx, run):
    r = np.arange(len(x))
    return x[r[:, None], idx[r % (8 * run) // run]]


E2M1 = np.array([0.0, 0.5, 1.0, 1.5, 2.0, 3.0, 4.0, 6.0, -0.0, -0.5, -1.0, -1.5, -2.0, -3.0, -4.0, -6.0])


def pack_weight(w, fmt):
    k, n = w.shape
    w = f64(np.asarray(w, np.float32).astype(ml_dtypes.bfloat16)).reshape(k // 32, 32, n)
    amax = np.abs(w).max(1)
    if fmt == "e4m3":
        byte = np.frexp(amax)[1] - 1 + 127 - 7
    else:
        mant, ex = np.frexp(amax / 6.0)
        byte = np.where(mant > 0.5, ex, ex - 1) + 127
    byte = np.clip(np.where(amax > 0, byte, 1), 1, 254)
    scaled = (w * np.exp2(127.0 - byte)[:, None, :]).reshape(k, n).astype(np.float32)
    by_word = np.ascontiguousarray(scaled.reshape(k // 512, 128, 4, n).transpose(0, 1, 3, 2))
    if fmt == "e4m3":
        words = by_word.astype(ml_dtypes.float8_e4m3fn).view(np.uint8)
    else:
        c = by_word.astype(ml_dtypes.float4_e2m1fn).view(np.uint8) & 0xF
        words = (c[..., 0::2] | (c[..., 1::2] << 4)).reshape(k // 512, 128, 2 * n)
    return np.ascontiguousarray(words), np.ascontiguousarray(byte.astype(np.uint8).reshape(k // 512, 16, n))


def unpack_weight(words, scales, fmt):
    g, _, n = scales.shape
    words = np.ascontiguousarray(words).reshape(g, 128, n, -1)
    if fmt == "e4m3":
        vals = words.view(ml_dtypes.float8_e4m3fn).astype(np.float64)
    else:
        nib = np.empty((g, 128, n, 4), np.uint8)
        nib[..., 0::2] = words & 0xF
        nib[..., 1::2] = words >> 4
        vals = E2M1[nib]
    vals = vals * np.repeat(np.exp2(scales.astype(np.float64) - 127.0), 8, axis=1)[..., None]
    return vals.transpose(0, 1, 3, 2).reshape(g * 512, n)


D, T, I, Q = 512, 1024, 512, 128


def setup_inputs():
    n = np.random.standard_normal
    idx = np.stack([np.random.permutation(T)[:I] for _ in range(8)])
    idx2 = np.stack([np.random.permutation(T)[:I] for _ in range(8)])
    idx3 = np.stack([np.random.permutation(T)[:I] for _ in range(8)])
    idx4 = np.stack([np.random.permutation(T)[:I] for _ in range(8)])
    fd = mx_kscale(D)
    keysp = pack_weight(n((D, T)) / fd[:, None], "e2m1")
    return {
        "query": (n((D, Q)) * 0.9 / np.sqrt(D) * fd[:, None]).astype(np.float32),
        "keys_words": keysp[0],
        "keys_scales": keysp[1],
        "lam": (np.random.uniform(0.3, 0.9, (Q, 1))).astype(np.float32),
        "old": (1.0 * n((Q, T))).astype(np.float32),
        "offs": striped8(idx),
        "offs2": striped8(idx2),
        "offs3": striped8(idx3),
        "offs4": striped8(idx4),
    }


def reference(query, keys_words, keys_scales, lam, old, offs, offs2, offs3, offs4):
    idx = unstriped8(offs)
    idx2 = unstriped8(offs2)
    idx3 = unstriped8(offs3)
    idx4 = unstriped8(offs4)
    keysu = unpack_weight(keys_words, keys_scales, "e2m1")
    queryq = mxq(f64(query), 0, "e4m3")
    a = queryq.T @ keysu
    w = pick8(a, idx, 16) + np.maximum(pick8(a, idx2, 16), pick8(a, idx3, 16)) * f64(lam)
    f1 = np.zeros((Q, T))
    f1[np.arange(Q)[:, None], idx4[np.arange(Q) % 128 // 16]] = w
    y = np.maximum(f1, f64(old)) + f64(old) * 0.25
    return y

@@ -1,0 +1,134 @@
+from contextlib import ExitStack
+
+import concourse.mybir as mybir
+
+D, T, I, Q = 512, 1024, 512, 128
+FLOPS = 2 * D * T * Q
+
+F32 = mybir.dt.float32
+BF16 = mybir.dt.bfloat16
+I32 = mybir.dt.int32
+U32 = mybir.dt.uint32
+U16 = mybir.dt.uint16
+U8 = mybir.dt.uint8
+FP8X4 = mybir.dt.float8_e4m3fn_x4
+FP4X4 = mybir.dt.float4_e2m1fn_x4
+ALU = mybir.AluOpType
+COPY = mybir.ActivationFunctionType.Copy
+
+P = 128
+PACK = 4
+GROUP = 16
+N_MM = 256
+HALF = I // 2
+N_OUT = 256
+
+
+def tile_attend_lookahead_lean_largerput_heads_kernel(
+    tc, query, keys_words, keys_scales, lam, old, offs, offs2, offs3, offs4, out
+):
+    nc = tc.nc
+    with ExitStack() as ctx:
+        keep = ctx.enter_context(tc.tile_pool(name="keep", bufs=1))
+        psum = ctx.enter_context(tc.psum_pool(name="psum", bufs=1))
+
+        k_scales = keep.tile([P, T], U8, align_bytes=64)
+        nc.vector.memset(k_scales[:].bitcast(U32), 0)
+
+        q_raw = keep.tile([P, PACK, Q], F32, tag="staged")
+        nc.sync.dma_start(q_raw[:], query.rearrange("(p j) q -> p j q", j=PACK))
+        k_words = keep.tile([P, 2 * T], U8, align_bytes=64)
+        nc.sync.dma_start(k_words[:].bitcast(I32), keys_words[0].bitcast(I32))
+        for quad in range(4):
+            nc.scalar.dma_start(
+                k_scales[32 * quad : 32 * quad + 4, :].bitcast(I32),
+                keys_scales[0, 4 * quad : 4 * quad + 4, :].bitcast(I32),
+            )
+        list2 = keep.tile([P, I // GROUP], U16)
+        nc.sync.dma_start(list2[:], offs2)
+        list3 = keep.tile([P, I // GROUP], U16)
+        nc.sync.dma_start(list3[:], offs3)
+        list1 = keep.tile([P, I // GROUP], U16)
+        nc.sync.dma_start(list1[:], offs)
+        list4 = keep.tile([P, I // GROUP], U16)
+        nc.sync.dma_start(list4[:], offs4)
+        lam_col = keep.tile([P, 1], F32)
+        nc.gpsimd.dma_start(lam_col[:], lam)
+
+        placed = keep.tile([P, T], F32)
+        nc.vector.memset(placed[:], 0.0)
+
+        q_bf = keep.tile([P, Q, PACK], BF16, align_bytes=64)
+        q_codes = keep.tile([P, Q], U32, align_bytes=64)
+        q_scales = keep.tile([P, Q], U8, align_bytes=64)
+        halves_q = [slice(0, Q // 2), slice(Q // 2, Q)]
+        for cols in halves_q:
+            nc.vector.tensor_copy(q_bf[:, cols, :], q_raw[:, :, cols].rearrange("p j q -> p q j"))
+        for cols in halves_q:
+            nc.vector.quantize_mx(
+                out=q_codes[:, cols].bitcast(FP8X4),
+                scales=q_scales[:, cols],
+                in_=q_bf[:, cols, :].rearrange("p q j -> p (q j)"),
+            )
+
+        old_sb = keep.tile([P, T], F32, tag="staged")
+        nc.sync.dma_start(old_sb[:], old)
+
+        scores = keep.tile([P, T], F32)
+        for b in range(T // N_MM):
+            cols = slice(b * N_MM, (b + 1) * N_MM)
+            bank = psum.tile([P, N_MM], F32, name="bank%d" % b)
+            nc.tensor.matmul_mx(
+                out=bank[:],
+                lhsT=q_codes[:].bitcast(FP8X4),
+                lhsT_scale=q_scales[:],
+                rhs=k_words[:, 2 * cols.start : 2 * cols.stop].bitcast(FP4X4),
+                rhs_scale=k_scales[:, cols],
+                start=True,
+                stop=True,
+            )
+            if b % 2 == 0:
+                nc.scalar.activation(scores[:, cols], bank[:], COPY)
+            else:
+                nc.vector.tensor_copy(scores[:, cols], bank[:])
+
+        halves = [slice(0, HALF), slice(HALF, I)]
+
+        def entries(listed, slots):
+            return listed[:, slots.start // GROUP : slots.stop // GROUP]
+
+        own = keep.tile([P, I], F32)
+        next2 = keep.tile([P, I], F32)
+        next3 = keep.tile([P, I], F32)
+        larger = keep.tile([P, I], F32)
+        lean = keep.tile([P, I], F32)
+        for slots in halves:
+            nc.vector.tensor_copy(next2[:, slots], scores[:].indirect(entries(list2, slots)))
+            nc.scalar.activation(next3[:, slots], scores[:].indirect(entries(list3, slots)), COPY)
+        for slots in halves:
+            nc.scalar.activation(own[:, slots], scores[:].indirect(entries(list1, slots)), COPY)
+        for slots in halves:
+            nc.vector.tensor_tensor(larger[:, slots], next2[:, slots], next3[:, slots], ALU.max)
+        for slots in halves:
+            nc.vector.tensor_scalar(lean[:, slots], larger[:, slots], lam_col[:], None, ALU.mult)
+        for slots in halves:
+            nc.vector.tensor_tensor(
+                placed[:].indirect(entries(list4, slots)), lean[:, slots], own[:, slots], ALU.add
+            )
+
+        kept = keep.tile([P, T], F32)
+        result = keep.tile([P, T], F32)
+        chunks = [slice(c * N_OUT, (c + 1) * N_OUT) for c in range(T // N_OUT)]
+
+        def take_larger(cols):
+            nc.vector.tensor_tensor(kept[:, cols], placed[:, cols], old_sb[:, cols], ALU.max)
+
+        take_larger(chunks[0])
+        for c, cols in enumerate(chunks):
+            if c + 1 < len(chunks):
+                take_larger(chunks[c + 1])
+            nc.vector.scalar_tensor_tensor(
+                result[:, cols], old_sb[:, cols], 0.25, kept[:, cols], ALU.mult, ALU.add
+            )
+            queue = nc.sync if c % 2 == 0 else nc.scalar
+            queue.dma_start(out[:, cols], result[:, cols])

@@ -19,9 +19,13 @@ COPY = mybir.ActivationFunctionType.Copy
 P = 128
 PACK = 4
 GROUP = 16
-N_MM = 256
+MM_WIDTHS = (256, 256, 256, 128, 128)
 HALF = I // 2
-N_OUT = 256
+OUT_WIDTHS = (320, 320, 256, 128)
+
+
+def runs(widths):
+    return [slice(sum(widths[:n]), sum(widths[: n + 1])) for n in range(len(widths))]
 
 
 def tile_attend_lookahead_lean_largerput_heads_kernel(
@@ -53,7 +57,7 @@ def tile_attend_lookahead_lean_largerput_heads_kernel(
         list4 = keep.tile([P, I // GROUP], U16)
         nc.sync.dma_start(list4[:], offs4)
         lam_col = keep.tile([P, 1], F32)
-        nc.gpsimd.dma_start(lam_col[:], lam)
+        nc.sync.dma_start(lam_col[:], lam)
 
         placed = keep.tile([P, T], F32)
         nc.vector.memset(placed[:], 0.0)
@@ -63,7 +67,10 @@ def tile_attend_lookahead_lean_largerput_heads_kernel(
         q_scales = keep.tile([P, Q], U8, align_bytes=64)
         halves_q = [slice(0, Q // 2), slice(Q // 2, Q)]
         for cols in halves_q:
-            nc.vector.tensor_copy(q_bf[:, cols, :], q_raw[:, :, cols].rearrange("p j q -> p q j"))
+            nc.vector.tensor_copy(
+                q_bf[:, cols, :].rearrange("p (c i) j -> p c j i", i=4),
+                q_raw[:, :, cols].rearrange("p j (c i) -> p c j i", i=4),
+            )
         for cols in halves_q:
             nc.vector.quantize_mx(
                 out=q_codes[:, cols].bitcast(FP8X4),
@@ -75,9 +82,8 @@ def tile_attend_lookahead_lean_largerput_heads_kernel(
         nc.sync.dma_start(old_sb[:], old)
 
         scores = keep.tile([P, T], F32)
-        for b in range(T // N_MM):
-            cols = slice(b * N_MM, (b + 1) * N_MM)
-            bank = psum.tile([P, N_MM], F32, name="bank%d" % b)
+        for b, cols in enumerate(runs(MM_WIDTHS)):
+            bank = psum.tile([P, cols.stop - cols.start], F32, name="bank%d" % b)
             nc.tensor.matmul_mx(
                 out=bank[:],
                 lhsT=q_codes[:].bitcast(FP8X4),
@@ -109,8 +115,9 @@ def tile_attend_lookahead_lean_largerput_heads_kernel(
             nc.scalar.activation(own[:, slots], scores[:].indirect(entries(list1, slots)), COPY)
         for slots in halves:
             nc.vector.tensor_tensor(larger[:, slots], next2[:, slots], next3[:, slots], ALU.max)
-        for slots in halves:
-            nc.vector.tensor_scalar(lean[:, slots], larger[:, slots], lam_col[:], None, ALU.mult)
+        first, second = halves
+        nc.vector.tensor_scalar(lean[:, first], larger[:, first], lam_col[:], None, ALU.mult)
+        nc.scalar.activation(lean[:, second], larger[:, second], COPY, scale=lam_col[:])
         for slots in halves:
             nc.vector.tensor_tensor(
                 placed[:].indirect(entries(list4, slots)), lean[:, slots], own[:, slots], ALU.add
@@ -118,7 +125,7 @@ def tile_attend_lookahead_lean_largerput_heads_kernel(
 
         kept = keep.tile([P, T], F32)
         result = keep.tile([P, T], F32)
-        chunks = [slice(c * N_OUT, (c + 1) * N_OUT) for c in range(T // N_OUT)]
+        chunks = runs(OUT_WIDTHS)
 
         def take_larger(cols):
             nc.vector.tensor_tensor(kept[:, cols], placed[:, cols], old_sb[:, cols], ALU.max)

@@ -106,18 +106,18 @@ def tile_attend_lookahead_lean_largerput_heads_kernel(
         own = keep.tile([P, I], F32)
         next2 = keep.tile([P, I], F32)
         next3 = keep.tile([P, I], F32)
-        larger = keep.tile([P, I], F32)
+        larger = keep.tile([P, HALF], F32)
         lean = keep.tile([P, I], F32)
         for slots in halves:
             nc.vector.tensor_copy(next2[:, slots], scores[:].indirect(entries(list2, slots)))
             nc.scalar.activation(next3[:, slots], scores[:].indirect(entries(list3, slots)), COPY)
         for slots in halves:
             nc.scalar.activation(own[:, slots], scores[:].indirect(entries(list1, slots)), COPY)
-        for slots in halves:
-            nc.vector.tensor_tensor(larger[:, slots], next2[:, slots], next3[:, slots], ALU.max)
         first, second = halves
-        nc.vector.tensor_scalar(lean[:, first], larger[:, first], lam_col[:], None, ALU.mult)
-        nc.scalar.activation(lean[:, second], larger[:, second], COPY, scale=lam_col[:])
+        nc.vector.tensor_tensor(larger[:], next2[:, first], next3[:, first], ALU.max)
+        nc.vector.tensor_scalar(lean[:, first], larger[:], lam_col[:], None, ALU.mult)
+        nc.vector.tensor_tensor(next2[:, first], next2[:, second], next3[:, second], ALU.max)
+        nc.scalar.activation(lean[:, second], next2[:, first], COPY, scale=lam_col[:])
         for slots in halves:
             nc.vector.tensor_tensor(
                 placed[:].indirect(entries(list4, slots)), lean[:, slots], own[:, slots], ALU.add

from contextlib import ExitStack

import concourse.mybir as mybir

D, T, I, Q = 512, 1024, 512, 128
FLOPS = 2 * D * T * Q

F32 = mybir.dt.float32
BF16 = mybir.dt.bfloat16
I32 = mybir.dt.int32
U32 = mybir.dt.uint32
U16 = mybir.dt.uint16
U8 = mybir.dt.uint8
FP8X4 = mybir.dt.float8_e4m3fn_x4
FP4X4 = mybir.dt.float4_e2m1fn_x4
ALU = mybir.AluOpType
COPY = mybir.ActivationFunctionType.Copy

P = 128
PACK = 4
GROUP = 16
MM_WIDTHS = (256, 256, 256, 128, 128)
HALF = I // 2
OUT_WIDTHS = (320, 320, 256, 128)


def runs(widths):
    return [slice(sum(widths[:n]), sum(widths[: n + 1])) for n in range(len(widths))]


def tile_attend_lookahead_lean_largerput_heads_kernel(
    tc, query, keys_words, keys_scales, lam, old, offs, offs2, offs3, offs4, out
):
    nc = tc.nc
    with ExitStack() as ctx:
        keep = ctx.enter_context(tc.tile_pool(name="keep", bufs=1))
        psum = ctx.enter_context(tc.psum_pool(name="psum", bufs=1))

        k_scales = keep.tile([P, T], U8, align_bytes=64)
        nc.vector.memset(k_scales[:].bitcast(U32), 0)

        q_raw = keep.tile([P, PACK, Q], F32, tag="staged")
        nc.sync.dma_start(q_raw[:], query.rearrange("(p j) q -> p j q", j=PACK))
        k_words = keep.tile([P, 2 * T], U8, align_bytes=64)
        nc.sync.dma_start(k_words[:].bitcast(I32), keys_words[0].bitcast(I32))
        for quad in range(4):
            nc.scalar.dma_start(
                k_scales[32 * quad : 32 * quad + 4, :].bitcast(I32),
                keys_scales[0, 4 * quad : 4 * quad + 4, :].bitcast(I32),
            )
        list2 = keep.tile([P, I // GROUP], U16)
        nc.sync.dma_start(list2[:], offs2)
        list3 = keep.tile([P, I // GROUP], U16)
        nc.sync.dma_start(list3[:], offs3)
        list1 = keep.tile([P, I // GROUP], U16)
        nc.sync.dma_start(list1[:], offs)
        list4 = keep.tile([P, I // GROUP], U16)
        nc.sync.dma_start(list4[:], offs4)
        lam_col = keep.tile([P, 1], F32)
        nc.sync.dma_start(lam_col[:], lam)

        placed = keep.tile([P, T], F32)
        nc.vector.memset(placed[:], 0.0)

        q_bf = keep.tile([P, Q, PACK], BF16, align_bytes=64)
        q_codes = keep.tile([P, Q], U32, align_bytes=64)
        q_scales = keep.tile([P, Q], U8, align_bytes=64)
        halves_q = [slice(0, Q // 2), slice(Q // 2, Q)]
        for cols in halves_q:
            nc.vector.tensor_copy(
                q_bf[:, cols, :].rearrange("p (c i) j -> p c j i", i=4),
                q_raw[:, :, cols].rearrange("p j (c i) -> p c j i", i=4),
            )
        for cols in halves_q:
            nc.vector.quantize_mx(
                out=q_codes[:, cols].bitcast(FP8X4),
                scales=q_scales[:, cols],
                in_=q_bf[:, cols, :].rearrange("p q j -> p (q j)"),
            )

        old_sb = keep.tile([P, T], F32, tag="staged")
        nc.sync.dma_start(old_sb[:], old)

        scores = keep.tile([P, T], F32)
        for b, cols in enumerate(runs(MM_WIDTHS)):
            bank = psum.tile([P, cols.stop - cols.start], F32, name="bank%d" % b)
            nc.tensor.matmul_mx(
                out=bank[:],
                lhsT=q_codes[:].bitcast(FP8X4),
                lhsT_scale=q_scales[:],
                rhs=k_words[:, 2 * cols.start : 2 * cols.stop].bitcast(FP4X4),
                rhs_scale=k_scales[:, cols],
                start=True,
                stop=True,
            )
            if b % 2 == 0:
                nc.scalar.activation(scores[:, cols], bank[:], COPY)
            else:
                nc.vector.tensor_copy(scores[:, cols], bank[:])

        halves = [slice(0, HALF), slice(HALF, I)]

        def entries(listed, slots):
            return listed[:, slots.start // GROUP : slots.stop // GROUP]

        own = keep.tile([P, I], F32)
        next2 = keep.tile([P, I], F32)
        next3 = keep.tile([P, I], F32)
        larger = keep.tile([P, HALF], F32)
        lean = keep.tile([P, I], F32)
        for slots in halves:
            nc.vector.tensor_copy(next2[:, slots], scores[:].indirect(entries(list2, slots)))
            nc.scalar.activation(next3[:, slots], scores[:].indirect(entries(list3, slots)), COPY)
        for slots in halves:
            nc.scalar.activation(own[:, slots], scores[:].indirect(entries(list1, slots)), COPY)
        first, second = halves
        nc.vector.tensor_tensor(larger[:], next2[:, first], next3[:, first], ALU.max)
        nc.vector.tensor_scalar(lean[:, first], larger[:], lam_col[:], None, ALU.mult)
        nc.vector.tensor_tensor(next2[:, first], next2[:, second], next3[:, second], ALU.max)
        nc.scalar.activation(lean[:, second], next2[:, first], COPY, scale=lam_col[:])
        for slots in halves:
            nc.vector.tensor_tensor(
                placed[:].indirect(entries(list4, slots)), lean[:, slots], own[:, slots], ALU.add
            )

        kept = keep.tile([P, T], F32)
        result = keep.tile([P, T], F32)
        chunks = runs(OUT_WIDTHS)

        def take_larger(cols):
            nc.vector.tensor_tensor(kept[:, cols], placed[:, cols], old_sb[:, cols], ALU.max)

        take_larger(chunks[0])
        for c, cols in enumerate(chunks):
            if c + 1 < len(chunks):
                take_larger(chunks[c + 1])
            nc.vector.scalar_tensor_tensor(
                result[:, cols], old_sb[:, cols], 0.25, kept[:, cols], ALU.mult, ALU.add
            )
            queue = nc.sync if c % 2 == 0 else nc.scalar
            queue.dma_start(out[:, cols], result[:, cols])
